import numpy as np
import ml_dtypes


def mxq(x, axis, fmt="e4m3"):
    dtype, down = {"e4m3": (ml_dtypes.float8_e4m3fn, 7), "e5m2": (ml_dtypes.float8_e5m2, 14)}[fmt]
    v = np.moveaxis(np.asarray(x, np.float32).astype(ml_dtypes.bfloat16).astype(np.float64), axis, -1)
    blocks = v.reshape(v.shape[:-1] + (-1, 32))
    amax = np.abs(blocks).max(-1, keepdims=True)
    byte = np.maximum(np.where(amax > 0, np.frexp(amax)[1] - 1 + 127, 0) - down, 1)
    scale = np.exp2(byte - 127.0)
    codes = (blocks / scale).astype(np.float32).astype(dtype).astype(np.float64)
    return np.moveaxis((codes * scale).reshape(v.shape), -1, axis)


WIDE = False


def mx_kscale(k):
    if not WIDE:
        return np.ones(k)
    levels = np.array([10, -10, 5, -5, 0])
    if k % 512:
        return np.exp2(np.random.permutation(np.resize(levels, k // 32))).repeat(32)
    a = np.empty((k // 512, 16))
    for p in range(k // 512):
        a[p, :8] = np.random.permutation(np.resize(levels, 8))
        for g in range(8):
            far = levels[np.abs(levels - a[p, g]) >= 10]
            a[p, g + 8] = far[np.random.randint(len(far))]
    return np.exp2(a.ravel()).repeat(32)


def f64(x):
    return np.asarray(x).astype(np.float64)


def striped(idx):
    return np.tile(np.asarray(idx).reshape(-1, 16).T, (8, 1)).astype(np.uint16)


def unstriped(offs):
    return offs[:16].T.reshape(-1).astype(np.int64)


E2M1 = np.array([0.0, 0.5, 1.0, 1.5, 2.0, 3.0, 4.0, 6.0, -0.0, -0.5, -1.0, -1.5, -2.0, -3.0, -4.0, -6.0])


def pack_weight(w, fmt):
    k, n = w.shape
    w = f64(np.asarray(w, np.float32).astype(ml_dtypes.bfloat16)).reshape(k // 32, 32, n)
    amax = np.abs(w).max(1)
    if fmt == "e4m3":
        byte = np.frexp(amax)[1] - 1 + 127 - 7
    else:
        mant, ex = np.frexp(amax / 6.0)
        byte = np.where(mant > 0.5, ex, ex - 1) + 127
    byte = np.clip(np.where(amax > 0, byte, 1), 1, 254)
    scaled = (w * np.exp2(127.0 - byte)[:, None, :]).reshape(k, n).astype(np.float32)
    by_word = np.ascontiguousarray(scaled.reshape(k // 512, 128, 4, n).transpose(0, 1, 3, 2))
    if fmt == "e4m3":
        words = by_word.astype(ml_dtypes.float8_e4m3fn).view(np.uint8)
    else:
        c = by_word.astype(ml_dtypes.float4_e2m1fn).view(np.uint8) & 0xF
        words = (c[..., 0::2] | (c[..., 1::2] << 4)).reshape(k // 512, 128, 2 * n)
    return np.ascontiguousarray(words), np.ascontiguousarray(byte.astype(np.uint8).reshape(k // 512, 16, n))


def unpack_weight(words, scales, fmt):
    g, _, n = scales.shape
    words = np.ascontiguousarray(words).reshape(g, 128, n, -1)
    if fmt == "e4m3":
        vals = words.view(ml_dtypes.float8_e4m3fn).astype(np.float64)
    else:
        nib = np.empty((g, 128, n, 4), np.uint8)
        nib[..., 0::2] = words & 0xF
        nib[..., 1::2] = words >> 4
        vals = E2M1[nib]
    vals = vals * np.repeat(np.exp2(scales.astype(np.float64) - 127.0), 8, axis=1)[..., None]
    return vals.transpose(0, 1, 3, 2).reshape(g * 512, n)


D, E, T, I, Q = 512, 512, 2048, 512, 128


def setup_inputs():
    n = np.random.standard_normal
    idx = np.random.permutation(T)[:I]
    fd = mx_kscale(D)
    fi = mx_kscale(I)
    ti = np.ones(T)
    ti[idx] = fi
    keysp = pack_weight(n((D, T)) / fd[:, None], "e4m3")
    return {
        "query": (n((D, Q)) * 0.4 / np.sqrt(D) * fd[:, None]).astype(np.float32),
        "keys_words": keysp[0],
        "keys_scales": keysp[1],
        "gain": (np.random.uniform(0.3, 0.8, (Q, 1))).astype(np.float32),
        "dquery": (n((D, Q)) * 0.6 / np.sqrt(D) * fd[:, None]).astype(np.float32),
        "os": (np.random.uniform(4.0, 16.0, (1, I)) * fi).astype(np.float32),
        "vals": (n((E, T)) / ti).astype(np.float32),
        "offs": striped(idx),
    }


def reference(query, keys_words, keys_scales, gain, dquery, os, vals, offs):
    idx = unstriped(offs)
    keysu = unpack_weight(keys_words, keys_scales, "e4m3")
    queryq = mxq(f64(query), 0, "e4m3")
    keysidxg = keysu[:, idx]
    a = queryq.T @ keysidxg
    dqueryq = mxq(f64(dquery), 0, "e4m3")
    ta = dqueryq.T @ keysidxg
    p = np.exp(a - np.max(a, axis=1, keepdims=True))
    z = np.sum(p, axis=1, keepdims=True)
    u1 = p / z * f64(gain) * 512.0
    p2 = np.exp(u1 - np.max(u1, axis=1, keepdims=True))
    z2 = np.sum(p2, axis=1, keepdims=True)
    tp = ta * p
    tz = np.sum(tp, axis=1, keepdims=True)
    tu1 = (tp - tz * p / z) / z * f64(gain) * 512.0
    tp2 = tu1 * p2
    tz2 = np.sum(tp2, axis=1, keepdims=True)
    tw = (tp2 - tz2 * p2 / z2) / z2
    wo1 = tw * f64(os)
    wt1 = wo1.T
    vt1 = f64(vals)[:, idx].T
    wt1q = mxq(wt1, 0, "e4m3")
    vt1q = mxq(vt1, 0, "e4m3")
    o = wt1q.T @ vt1q
    return o

@@ -1,0 +1,159 @@
+from contextlib import ExitStack
+
+import concourse.mybir as mybir
+from concourse.masks import make_identity
+
+D, E, T, I, Q = 512, 512, 2048, 512, 128
+FLOPS = 2 * (2 * D * Q * I + I * Q * E)
+
+F32 = mybir.dt.float32
+BF16 = mybir.dt.bfloat16
+I32 = mybir.dt.int32
+U32 = mybir.dt.uint32
+U16 = mybir.dt.uint16
+U8 = mybir.dt.uint8
+FP8X4 = mybir.dt.float8_e4m3fn_x4
+ALU = mybir.AluOpType
+ACT = mybir.ActivationFunctionType
+AXIS = mybir.AxisListType
+
+P = 128
+PACK = 4
+
+
+def tile_attend_ttdoubled_kernel(tc, query, keys_words, keys_scales, gain, dquery, slot_factor, vals, offs, out):
+    nc = tc.nc
+    with ExitStack() as ctx:
+        held = ctx.enter_context(tc.tile_pool(name="held", bufs=1))
+        psum = ctx.enter_context(tc.psum_pool(name="psum", bufs=1))
+
+        offsets = held.tile([P, I // 16], U16, name="offsets")
+        nc.sync.dma_start(offsets[:], offs)
+
+        scale_pool = held.tile([P, T], U8, name="scale_pool")
+        nc.gpsimd.memset(scale_pool[:].bitcast(I32), 0)
+        for quad in range(4):
+            nc.scalar.dma_start(
+                scale_pool[32 * quad : 32 * quad + 4, :].bitcast(I32),
+                keys_scales[0, 4 * quad : 4 * quad + 4, :].bitcast(I32),
+            )
+        word_pool = held.tile([P, T], U32, name="word_pool")
+        nc.sync.dma_start(word_pool[:].bitcast(I32), keys_words[0].rearrange("p n t -> p (n t)").bitcast(I32))
+
+        raw = []
+        for name, src in (("q", query), ("dq", dquery)):
+            t = held.tile([P, PACK, Q], F32, name=name + "_raw")
+            nc.sync.dma_start(t[:], src.rearrange("(p j) w -> p j w", j=PACK))
+            raw.append(t)
+
+        gain_col = held.tile([P, 1], F32, name="gain_col")
+        nc.sync.dma_start(gain_col[:], gain)
+        factor = held.tile([P, PACK], F32, name="factor")
+        val_pools = []
+        for j in range(E // P):
+            t = held.tile([P, T], F32, name="val_pool%d" % j)
+            nc.sync.dma_start(t[:], vals[j * P : (j + 1) * P, :])
+            val_pools.append(t)
+            if j == 0:
+                nc.sync.dma_start(factor[:], slot_factor.rearrange("o (p t) -> (o p) t", t=PACK))
+
+        ident = held.tile([P, P], F32, name="ident")
+        make_identity(nc, ident[:])
+
+        warm = held.tile([P, 1], F32, name="warm")
+        nc.scalar.activation(warm[:], ident[:, 0:1], ACT.Exp)
+
+        key_scales = held.tile([P, I], U8, name="key_scales", align_bytes=64)
+        nc.vector.tensor_copy(key_scales[:], scale_pool[:].indirect(offsets[:]))
+        key_words = held.tile([P, I], U32, name="key_words", align_bytes=64)
+        nc.vector.tensor_copy(key_words[:], word_pool[:].indirect(offsets[:]))
+
+        scores = []
+        for name, t in zip(("q", "dq"), raw):
+            grouped = held.tile([P, Q, PACK], BF16, name=name + "_grouped", align_bytes=64)
+            nc.scalar.copy(
+                grouped[:].rearrange("p (c i) t -> p c t i", i=4),
+                t[:].rearrange("p t (c i) -> p c t i", i=4),
+            )
+            codes = held.tile([P, Q], U32, name=name + "_codes", align_bytes=64)
+            scales = held.tile([P, Q], U8, name=name + "_scales", align_bytes=64)
+            nc.vector.quantize_mx(codes[:].bitcast(FP8X4), scales[:], grouped[:].rearrange("p w j -> p (w j)"))
+            bank = psum.tile([P, I], F32, name=name + "_bank")
+            nc.tensor.matmul_mx(
+                out=bank[:], lhsT=codes[:].bitcast(FP8X4), lhsT_scale=scales[:],
+                rhs=key_words[:].bitcast(FP8X4), rhs_scale=key_scales[:], start=True, stop=True,
+            )
+            scores.append(bank[:].rearrange("p (s r) -> p r s", r=PACK))
+        a, ta = scores
+
+        def wide(name):
+            return held.tile([P, PACK, P], F32, name=name)
+
+        def col(name, n=1):
+            return held.tile([P, n], F32, name=name)
+
+        neg_a, neg_max = wide("neg_a"), col("neg_max")
+        nc.vector.tensor_scalar(neg_a[:], a, -1.0, None, ALU.mult, ALU.min, accum_out=neg_max[:])
+        p, z = wide("p"), col("z")
+        nc.scalar.activation(p[:], neg_a[:], ACT.Exp, bias=neg_max[:], scale=-1.0, accum_out=z[:])
+        neg_min, p_min = col("neg_min"), col("p_min")
+        nc.vector.tensor_reduce(neg_min[:], neg_a[:].rearrange("p r s -> p (r s)"), AXIS.X, ALU.max)
+        nc.scalar.activation(p_min[:], neg_min[:], ACT.Exp, bias=neg_max[:], scale=-1.0)
+
+        c = col("c", 2)
+        neg_c = col("neg_c")
+        nc.vector.tensor_scalar(c[:, 0:1], gain_col[:], float(I), None, ALU.mult)
+        nc.vector.tensor_scalar(neg_c[:], gain_col[:], -float(I), None, ALU.mult)
+        nc.vector.tensor_scalar(c[:, 1:2], p_min[:], neg_c[:], neg_c[:], ALU.mult, ALU.min)
+        rz, s = col("rz"), col("s", 2)
+        nc.vector.reciprocal(rz[:], z[:])
+        nc.vector.tensor_scalar(s[:], c[:], rz[:], None, ALU.mult)
+        p2, z2 = wide("p2"), col("z2")
+        nc.scalar.activation(p2[:], p[:], ACT.Exp, bias=s[:, 1:2], scale=s[:, 0:1], accum_out=z2[:])
+
+        tp, mu = wide("tp"), col("mu")
+        nc.vector.scalar_tensor_tensor(tp[:], ta, rz[:], p[:], ALU.mult, ALU.mult, accum_out=mu[:])
+        g = wide("g")
+        nc.vector.scalar_tensor_tensor(g[:], ta, mu[:], p[:], ALU.subtract, ALU.mult)
+        rz2, k = col("rz2"), col("k")
+        nc.vector.reciprocal(rz2[:], z2[:])
+        nc.vector.tensor_scalar(k[:], rz2[:], s[:, 0:1], None, ALU.mult)
+        big, h = wide("big"), col("h")
+        nc.vector.scalar_tensor_tensor(big[:], g[:], k[:], p2[:], ALU.mult, ALU.mult, accum_out=h[:])
+        nr = col("nr")
+        nc.vector.tensor_scalar(nr[:], h[:], rz2[:], -1.0, ALU.mult, ALU.mult)
+        tw = wide("tw")
+        nc.vector.scalar_tensor_tensor(tw[:], p2[:], nr[:], big[:], ALU.mult, ALU.add)
+
+        tw_bank = psum.tile([P, PACK, Q], F32, name="tw_bank")
+        for r in range(PACK):
+            nc.tensor.transpose(tw_bank[:, r, :], tw[:, r, :], ident[:])
+        w_grouped = held.tile([P, Q, PACK], BF16, name="w_grouped", align_bytes=64)
+        nc.vector.tensor_tensor(
+            w_grouped[:], tw_bank[:].rearrange("p r q -> p q r"),
+            factor[:].unsqueeze(1).to_broadcast([P, Q, PACK]), ALU.mult,
+        )
+        w_codes = held.tile([P, Q], U32, name="w_codes", align_bytes=64)
+        w_scales = held.tile([P, Q], U8, name="w_scales", align_bytes=64)
+        nc.vector.quantize_mx(w_codes[:].bitcast(FP8X4), w_scales[:], w_grouped[:].rearrange("p w j -> p (w j)"))
+
+        for j in range(E // P):
+            picked = held.tile([P, I], BF16, name="picked%d" % j)
+            nc.vector.tensor_copy(picked[:], val_pools[j][:].indirect(offsets[:]))
+            words = picked[:].bitcast(F32)
+            turned = psum.tile([P, 2, P], F32, name="turned", tag="turned", bufs=2)
+            for u in range(2):
+                nc.tensor.transpose(turned[:, u, :], words[:, u : I // 2 : 2], ident[:])
+            v_grouped = held.tile([P, P, PACK], BF16, name="v_grouped%d" % j, align_bytes=64)
+            nc.scalar.copy(v_grouped[:].bitcast(F32), turned[:].rearrange("p u e -> p e u"))
+            v_codes = held.tile([P, P], U32, name="v_codes%d" % j, align_bytes=64)
+            v_scales = held.tile([P, P], U8, name="v_scales%d" % j, align_bytes=64)
+            nc.vector.quantize_mx(v_codes[:].bitcast(FP8X4), v_scales[:], v_grouped[:].rearrange("p w j -> p (w j)"))
+            acc = psum.tile([P, P], F32, name="acc", tag="acc", bufs=3)
+            nc.tensor.matmul_mx(
+                out=acc[:], lhsT=w_codes[:].bitcast(FP8X4), lhsT_scale=w_scales[:],
+                rhs=v_codes[:].bitcast(FP8X4), rhs_scale=v_scales[:], start=True, stop=True,
+            )
+            result = held.tile([P, P], F32, name="result%d" % j)
+            nc.scalar.copy(result[:], acc[:])
+            nc.sync.dma_start(out[:, j * P : (j + 1) * P], result[:])

@@ -27,46 +27,49 @@ def tile_attend_ttdoubled_kernel(tc, query, keys_words, keys_scales, gain, dquer
         held = ctx.enter_context(tc.tile_pool(name="held", bufs=1))
         psum = ctx.enter_context(tc.psum_pool(name="psum", bufs=1))
 
+        scale_rows = held.tile([P, T // 4], I32, name="scale_rows")
+        for quad in range(4):
+            nc.sync.dma_start(
+                scale_rows[32 * quad : 32 * quad + 4, :],
+                keys_scales[0, 4 * quad : 4 * quad + 4, :].bitcast(I32),
+            )
         offsets = held.tile([P, I // 16], U16, name="offsets")
         nc.sync.dma_start(offsets[:], offs)
 
         scale_pool = held.tile([P, T], U8, name="scale_pool")
-        nc.gpsimd.memset(scale_pool[:].bitcast(I32), 0)
+        nc.vector.memset(scale_pool[:].bitcast(I32), 0)
         for quad in range(4):
-            nc.scalar.dma_start(
-                scale_pool[32 * quad : 32 * quad + 4, :].bitcast(I32),
-                keys_scales[0, 4 * quad : 4 * quad + 4, :].bitcast(I32),
-            )
-        word_pool = held.tile([P, T], U32, name="word_pool")
-        nc.sync.dma_start(word_pool[:].bitcast(I32), keys_words[0].rearrange("p n t -> p (n t)").bitcast(I32))
-
+            rows = slice(32 * quad, 32 * quad + 4)
+            nc.vector.tensor_copy(scale_pool[rows, :].bitcast(I32), scale_rows[rows, :])
         raw = []
-        for name, src in (("q", query), ("dq", dquery)):
+        for name, src, tag in (("q", query, "slot2"), ("dq", dquery, "slot3")):
             t = held.tile([P, PACK, Q], F32, name=name + "_raw")
             nc.sync.dma_start(t[:], src.rearrange("(p j) w -> p j w", j=PACK))
             raw.append(t)
+            if name == "q":
+                word_pool = held.tile([P, T], U32, name="word_pool")
+                nc.sync.dma_start(word_pool[:].bitcast(I32), keys_words[0].rearrange("p n t -> p (n t)").bitcast(I32))
 
         gain_col = held.tile([P, 1], F32, name="gain_col")
         nc.sync.dma_start(gain_col[:], gain)
         factor = held.tile([P, PACK], F32, name="factor")
-        val_pools = []
-        for j in range(E // P):
-            t = held.tile([P, T], F32, name="val_pool%d" % j)
-            nc.sync.dma_start(t[:], vals[j * P : (j + 1) * P, :])
-            val_pools.append(t)
-            if j == 0:
-                nc.sync.dma_start(factor[:], slot_factor.rearrange("o (p t) -> (o p) t", t=PACK))
 
         ident = held.tile([P, P], F32, name="ident")
         make_identity(nc, ident[:])
 
+        s = held.tile([P, 3], F32, name="s")
+        nc.vector.memset(s[:, 2:3], -1.0)
         warm = held.tile([P, 1], F32, name="warm")
-        nc.scalar.activation(warm[:], ident[:, 0:1], ACT.Exp)
+        nc.scalar.activation(warm[:], s[:, 2:3], ACT.Exp)
 
         key_scales = held.tile([P, I], U8, name="key_scales", align_bytes=64)
         nc.vector.tensor_copy(key_scales[:], scale_pool[:].indirect(offsets[:]))
-        key_words = held.tile([P, I], U32, name="key_words", align_bytes=64)
-        nc.vector.tensor_copy(key_words[:], word_pool[:].indirect(offsets[:]))
+        H = I // 2
+        key_words = []
+        for half in range(2):
+            t = held.tile([P, H], U32, name="key_words%d" % half, align_bytes=64)
+            nc.vector.tensor_copy(t[:], word_pool[:].indirect(offsets[:, half * H // 16 : (half + 1) * H // 16]))
+            key_words.append(t)
 
         scores = []
         for name, t in zip(("q", "dq"), raw):
@@ -78,13 +81,28 @@ def tile_attend_ttdoubled_kernel(tc, query, keys_words, keys_scales, gain, dquer
             codes = held.tile([P, Q], U32, name=name + "_codes", align_bytes=64)
             scales = held.tile([P, Q], U8, name=name + "_scales", align_bytes=64)
             nc.vector.quantize_mx(codes[:].bitcast(FP8X4), scales[:], grouped[:].rearrange("p w j -> p (w j)"))
-            bank = psum.tile([P, I], F32, name=name + "_bank")
-            nc.tensor.matmul_mx(
-                out=bank[:], lhsT=codes[:].bitcast(FP8X4), lhsT_scale=scales[:],
-                rhs=key_words[:].bitcast(FP8X4), rhs_scale=key_scales[:], start=True, stop=True,
-            )
-            scores.append(bank[:].rearrange("p (s r) -> p r s", r=PACK))
-        a, ta = scores
+            if name == "q":
+                halves = [psum.tile([P, H], F32, name="a%d" % n, tag="bank%d" % n)[:] for n in range(2)]
+                scores.extend(b.rearrange("p (s r) -> p r s", r=PACK) for b in halves)
+            else:
+                bank = psum.tile([P, I], F32, name="ta", tag="bank2")
+                halves = [bank[:, n * H : (n + 1) * H] for n in range(2)]
+                scores.append(bank[:].rearrange("p (s r) -> p r s", r=PACK))
+            for n in range(2):
+                nc.tensor.matmul_mx(
+                    out=halves[n], lhsT=codes[:].bitcast(FP8X4), lhsT_scale=scales[:],
+                    rhs=key_words[n][:].bitcast(FP8X4), rhs_scale=key_scales[:, n * H : (n + 1) * H],
+                    start=True, stop=True,
+                )
+        a0, a1, ta = scores
+
+        val_pools = []
+        for j in range(E // P):
+            t = held.tile([P, T], F32, name="val_pool%d" % j, tag="slot%d" % j, align_bytes=64)
+            nc.sync.dma_start(t[:], vals[j * P : (j + 1) * P, :])
+            val_pools.append(t)
+            if j == 0:
+                nc.sync.dma_start(factor[:], slot_factor.rearrange("o (p t) -> (o p) t", t=PACK))
 
         def wide(name):
             return held.tile([P, PACK, P], F32, name=name)
@@ -92,68 +110,88 @@ def tile_attend_ttdoubled_kernel(tc, query, keys_words, keys_scales, gain, dquer
         def col(name, n=1):
             return held.tile([P, n], F32, name=name)
 
-        neg_a, neg_max = wide("neg_a"), col("neg_max")
-        nc.vector.tensor_scalar(neg_a[:], a, -1.0, None, ALU.mult, ALU.min, accum_out=neg_max[:])
-        p, z = wide("p"), col("z")
-        nc.scalar.activation(p[:], neg_a[:], ACT.Exp, bias=neg_max[:], scale=-1.0, accum_out=z[:])
-        neg_min, p_min = col("neg_min"), col("p_min")
-        nc.vector.tensor_reduce(neg_min[:], neg_a[:].rearrange("p r s -> p (r s)"), AXIS.X, ALU.max)
-        nc.scalar.activation(p_min[:], neg_min[:], ACT.Exp, bias=neg_max[:], scale=-1.0)
-
-        c = col("c", 2)
-        neg_c = col("neg_c")
-        nc.vector.tensor_scalar(c[:, 0:1], gain_col[:], float(I), None, ALU.mult)
-        nc.vector.tensor_scalar(neg_c[:], gain_col[:], -float(I), None, ALU.mult)
-        nc.vector.tensor_scalar(c[:, 1:2], p_min[:], neg_c[:], neg_c[:], ALU.mult, ALU.min)
-        rz, s = col("rz"), col("s", 2)
-        nc.vector.reciprocal(rz[:], z[:])
-        nc.vector.tensor_scalar(s[:], c[:], rz[:], None, ALU.mult)
-        p2, z2 = wide("p2"), col("z2")
-        nc.scalar.activation(p2[:], p[:], ACT.Exp, bias=s[:, 1:2], scale=s[:, 0:1], accum_out=z2[:])
-
-        tp, mu = wide("tp"), col("mu")
-        nc.vector.scalar_tensor_tensor(tp[:], ta, rz[:], p[:], ALU.mult, ALU.mult, accum_out=mu[:])
-        g = wide("g")
-        nc.vector.scalar_tensor_tensor(g[:], ta, mu[:], p[:], ALU.subtract, ALU.mult)
-        rz2, k = col("rz2"), col("k")
-        nc.vector.reciprocal(rz2[:], z2[:])
-        nc.vector.tensor_scalar(k[:], rz2[:], s[:, 0:1], None, ALU.mult)
-        big, h = wide("big"), col("h")
-        nc.vector.scalar_tensor_tensor(big[:], g[:], k[:], p2[:], ALU.mult, ALU.mult, accum_out=h[:])
-        nr = col("nr")
-        nc.vector.tensor_scalar(nr[:], h[:], rz2[:], -1.0, ALU.mult, ALU.mult)
-        tw = wide("tw")
-        nc.vector.scalar_tensor_tensor(tw[:], p2[:], nr[:], big[:], ALU.mult, ALU.add)
-
-        tw_bank = psum.tile([P, PACK, Q], F32, name="tw_bank")
-        for r in range(PACK):
-            nc.tensor.transpose(tw_bank[:, r, :], tw[:, r, :], ident[:])
-        w_grouped = held.tile([P, Q, PACK], BF16, name="w_grouped", align_bytes=64)
-        nc.vector.tensor_tensor(
-            w_grouped[:], tw_bank[:].rearrange("p r q -> p q r"),
-            factor[:].unsqueeze(1).to_broadcast([P, Q, PACK]), ALU.mult,
-        )
-        w_codes = held.tile([P, Q], U32, name="w_codes", align_bytes=64)
-        w_scales = held.tile([P, Q], U8, name="w_scales", align_bytes=64)
-        nc.vector.quantize_mx(w_codes[:].bitcast(FP8X4), w_scales[:], w_grouped[:].rearrange("p w j -> p (w j)"))
-
-        for j in range(E // P):
-            picked = held.tile([P, I], BF16, name="picked%d" % j)
+        def turn_values(j, grouped, tag):
+            picked = held.tile([P, I], BF16, name="picked%d" % j, tag=tag, align_bytes=64)
             nc.vector.tensor_copy(picked[:], val_pools[j][:].indirect(offsets[:]))
             words = picked[:].bitcast(F32)
             turned = psum.tile([P, 2, P], F32, name="turned", tag="turned", bufs=2)
             for u in range(2):
                 nc.tensor.transpose(turned[:, u, :], words[:, u : I // 2 : 2], ident[:])
-            v_grouped = held.tile([P, P, PACK], BF16, name="v_grouped%d" % j, align_bytes=64)
-            nc.scalar.copy(v_grouped[:].bitcast(F32), turned[:].rearrange("p u e -> p e u"))
-            v_codes = held.tile([P, P], U32, name="v_codes%d" % j, align_bytes=64)
-            v_scales = held.tile([P, P], U8, name="v_scales%d" % j, align_bytes=64)
-            nc.vector.quantize_mx(v_codes[:].bitcast(FP8X4), v_scales[:], v_grouped[:].rearrange("p w j -> p (w j)"))
-            acc = psum.tile([P, P], F32, name="acc", tag="acc", bufs=3)
-            nc.tensor.matmul_mx(
-                out=acc[:], lhsT=w_codes[:].bitcast(FP8X4), lhsT_scale=w_scales[:],
-                rhs=v_codes[:].bitcast(FP8X4), rhs_scale=v_scales[:], start=True, stop=True,
-            )
-            result = held.tile([P, P], F32, name="result%d" % j)
+            nc.scalar.copy(grouped.bitcast(F32), turned[:].rearrange("p u e -> p e u"))
+
+        def quantise(codes, grouped, name):
+            scales = held.tile([P, codes.shape[1]], U8, name=name + "_scales", align_bytes=64)
+            nc.vector.quantize_mx(codes.bitcast(FP8X4), scales[:], grouped.rearrange("p w j -> p (w j)"))
+            return codes, scales
+
+        c, neg_c = col("c", 2), col("neg_c")
+        nc.vector.tensor_scalar(c[:, 1:2], gain_col[:], float(I), None, ALU.mult)
+        nc.vector.tensor_scalar(neg_c[:], gain_col[:], -float(I), None, ALU.mult)
+
+        neg_a, neg_max0, neg_max = wide("neg_a"), col("neg_max0"), col("neg_max")
+        nc.vector.tensor_scalar(neg_a[:, :, 0 : P // 2], a0, -1.0, None, ALU.mult, ALU.min, accum_out=neg_max0[:])
+        nc.vector.tensor_scalar(neg_a[:, :, P // 2 : P], a1, -1.0, neg_max0[:], ALU.mult, ALU.min, accum_out=neg_max[:])
+        p, z = wide("p"), col("z")
+        nc.scalar.activation(p[:], neg_a[:], ACT.Exp, bias=neg_max[:], scale=-1.0, accum_out=z[:])
+
+        v01 = held.tile([P, 2 * P, PACK], BF16, name="v01", align_bytes=64)
+        v2 = held.tile([P, P, PACK], BF16, name="v2", align_bytes=64)
+        v3 = held.tile([P, P, PACK], BF16, name="v3", align_bytes=64)
+        turn_values(0, v01[:, 0:P, :], "picked0")
+
+        scratch = held.tile([P, I + 8], F32, name="scratch", tag="slot0", align_bytes=64)
+        junk = scratch[:, 0:I].rearrange("p (r s) -> p r s", r=PACK)
+        rz = scratch[:, I : I + 1]
+        nc.vector.reciprocal(rz, z[:])
+        nc.vector.tensor_scalar(junk, p[:], neg_c[:], None, ALU.mult, ALU.min, accum_out=c[:, 0:1])
+        nc.scalar.activation(s[:, 0:2], c[:], ACT.Identity, scale=rz)
+        p2, z2 = wide("p2"), col("z2")
+        nc.scalar.activation(p2[:], p[:], ACT.Exp, bias=s[:, 0:1], scale=s[:, 1:2], accum_out=z2[:])
+
+        tp, mu = wide("tp"), col("mu")
+        nc.vector.scalar_tensor_tensor(tp[:], ta, rz, p[:], ALU.mult, ALU.mult, accum_out=mu[:])
+        g = held.tile([P, PACK, P], F32, name="g", tag="g", align_bytes=64)
+        nc.vector.scalar_tensor_tensor(g[:], ta, mu[:], p[:], ALU.subtract, ALU.mult)
+        rz2, k = col("rz2"), col("k", 2)
+        nc.vector.reciprocal(rz2[:], z2[:])
+        nc.vector.tensor_scalar(k[:], s[:, 1:3], rz2[:], None, ALU.mult)
+        big, h = wide("big"), col("h")
+        nc.vector.scalar_tensor_tensor(big[:], g[:], k[:, 0:1], p2[:], ALU.mult, ALU.mult, accum_out=h[:])
+        nr = col("nr")
+        nc.scalar.activation(nr[:], h[:], ACT.Identity, scale=k[:, 1:2])
+        corr = wide("corr")
+        tw_banks = [psum.tile([P, Q], F32, name="tw%d" % r, tag="bank%d" % r) for r in range(PACK)]
+        for r in range(PACK):
+            nc.tensor.matmul(tw_banks[r][:], big[:, r, :], ident[:], start=True, stop=False, is_transpose=True)
+        for r in range(PACK):
+            nc.scalar.activation(corr[:, r, :], p2[:, r, :], ACT.Identity, scale=nr[:])
+            nc.tensor.matmul(tw_banks[r][:], corr[:, r, :], ident[:], start=False, stop=True, is_transpose=True)
+        w_grouped = held.tile([P, Q, PACK], BF16, name="w_grouped", align_bytes=64)
+        for r in range(PACK):
+            nc.scalar.activation(w_grouped[:, :, r], tw_banks[r][:], ACT.Identity, scale=factor[:, r : r + 1])
+
+        turn_values(1, v01[:, P : 2 * P, :], "g")
+        turn_values(2, v2[:], "picked2")
+        turn_values(3, v3[:], "picked3")
+        codes = held.tile([P, 5 * P], U32, name="late_codes", tag="slot3", align_bytes=64)
+        v01_ops = quantise(codes[:, 0 : 2 * P], v01[:], "v01")
+        w_codes, w_scales = quantise(codes[:, 2 * P : 3 * P], w_grouped[:], "w")
+        v2_ops = quantise(codes[:, 3 * P : 4 * P], v2[:], "v2")
+        v3_ops = quantise(codes[:, 4 * P : 5 * P], v3[:], "v3")
+
+        e0 = 0
+        for name, parts in (("first", (v01_ops, v2_ops)), ("last", (v3_ops,))):
+            width = sum(part[0].shape[1] for part in parts)
+            acc = psum.tile([P, width], F32, name="acc_" + name)
+            n0 = 0
+            for v_codes, v_scales in parts:
+                n1 = n0 + v_codes.shape[1]
+                nc.tensor.matmul_mx(
+                    out=acc[:, n0:n1], lhsT=w_codes.bitcast(FP8X4), lhsT_scale=w_scales[:],
+                    rhs=v_codes.bitcast(FP8X4), rhs_scale=v_scales[:], start=True, stop=True,
+                )
+                n0 = n1
+            result = held.tile([P, width], F32, name="result_" + name)
             nc.scalar.copy(result[:], acc[:])
-            nc.sync.dma_start(out[:, j * P : (j + 1) * P], result[:])
+            nc.sync.dma_start(out[:, e0 : e0 + width], result[:])
+            e0 = e0 + width

@@ -15,10 +15,14 @@ U8 = mybir.dt.uint8
 FP8X4 = mybir.dt.float8_e4m3fn_x4
 ALU = mybir.AluOpType
 ACT = mybir.ActivationFunctionType
-AXIS = mybir.AxisListType
 
 P = 128
 PACK = 4
+QUADRANT = 32
+LIST_ROWS = 16
+HALF = I // 2
+VALUE_TILES = E // P
+MX_ALIGN = 64
 
 
 def tile_attend_ttdoubled_kernel(tc, query, keys_words, keys_scales, gain, dquery, slot_factor, vals, offs, out):
@@ -27,171 +31,170 @@ def tile_attend_ttdoubled_kernel(tc, query, keys_words, keys_scales, gain, dquer
         held = ctx.enter_context(tc.tile_pool(name="held", bufs=1))
         psum = ctx.enter_context(tc.psum_pool(name="psum", bufs=1))
 
+        def dealt(name):
+            return held.tile([P, PACK, P], F32, name=name)
+
+        def column(name, n=1):
+            return held.tile([P, n], F32, name=name)
+
+        def quantise(codes, grouped, name):
+            scales = held.tile([P, codes.shape[1]], U8, name=name + "_scales", align_bytes=MX_ALIGN)
+            nc.vector.quantize_mx(codes.bitcast(FP8X4), scales[:], grouped.rearrange("p c r -> p (c r)"))
+            return codes, scales[:]
+
+        def product(acc, stationary, moving):
+            nc.tensor.matmul_mx(
+                out=acc, lhsT=stationary[0].bitcast(FP8X4), lhsT_scale=stationary[1],
+                rhs=moving[0].bitcast(FP8X4), rhs_scale=moving[1], start=True, stop=True,
+            )
+
         scale_rows = held.tile([P, T // 4], I32, name="scale_rows")
-        for quad in range(4):
-            nc.sync.dma_start(
-                scale_rows[32 * quad : 32 * quad + 4, :],
+        for quad in range(P // QUADRANT):
+            (nc.sync, nc.scalar)[quad % 2].dma_start(
+                scale_rows[QUADRANT * quad : QUADRANT * quad + 4, :],
                 keys_scales[0, 4 * quad : 4 * quad + 4, :].bitcast(I32),
             )
-        offsets = held.tile([P, I // 16], U16, name="offsets")
+        offsets = held.tile([P, I // LIST_ROWS], U16, name="offsets")
         nc.sync.dma_start(offsets[:], offs)
 
         scale_pool = held.tile([P, T], U8, name="scale_pool")
         nc.vector.memset(scale_pool[:].bitcast(I32), 0)
-        for quad in range(4):
-            rows = slice(32 * quad, 32 * quad + 4)
+        for quad in range(P // QUADRANT):
+            rows = slice(QUADRANT * quad, QUADRANT * quad + 4)
             nc.vector.tensor_copy(scale_pool[rows, :].bitcast(I32), scale_rows[rows, :])
-        raw = []
-        for name, src, tag in (("q", query, "slot2"), ("dq", dquery, "slot3")):
-            t = held.tile([P, PACK, Q], F32, name=name + "_raw")
-            nc.sync.dma_start(t[:], src.rearrange("(p j) w -> p j w", j=PACK))
-            raw.append(t)
-            if name == "q":
-                word_pool = held.tile([P, T], U32, name="word_pool")
-                nc.sync.dma_start(word_pool[:].bitcast(I32), keys_words[0].rearrange("p n t -> p (n t)").bitcast(I32))
 
-        gain_col = held.tile([P, 1], F32, name="gain_col")
+        query_raw = held.tile([P, PACK, Q], F32, name="query_raw")
+        nc.sync.dma_start(query_raw[:], query.rearrange("(p r) c -> p r c", r=PACK))
+        word_pool = held.tile([P, T], U32, name="word_pool")
+        nc.sync.dma_start(word_pool[:].bitcast(I32), keys_words[0].rearrange("p n r -> p (n r)").bitcast(I32))
+        dquery_raw = held.tile([P, PACK, Q], F32, name="dquery_raw")
+        nc.sync.dma_start(dquery_raw[:], dquery.rearrange("(p r) c -> p r c", r=PACK))
+        gain_col = column("gain_col")
         nc.sync.dma_start(gain_col[:], gain)
-        factor = held.tile([P, PACK], F32, name="factor")
 
         ident = held.tile([P, P], F32, name="ident")
         make_identity(nc, ident[:])
 
-        s = held.tile([P, 3], F32, name="s")
-        nc.vector.memset(s[:, 2:3], -1.0)
-        warm = held.tile([P, 1], F32, name="warm")
-        nc.scalar.activation(warm[:], s[:, 2:3], ACT.Exp)
+        row_terms = column("row_terms", 3)
+        nc.vector.memset(row_terms[:, 2:3], -1.0)
 
-        key_scales = held.tile([P, I], U8, name="key_scales", align_bytes=64)
+        key_scales = held.tile([P, I], U8, name="key_scales", align_bytes=MX_ALIGN)
         nc.vector.tensor_copy(key_scales[:], scale_pool[:].indirect(offsets[:]))
-        H = I // 2
-        key_words = []
+        keys = []
         for half in range(2):
-            t = held.tile([P, H], U32, name="key_words%d" % half, align_bytes=64)
-            nc.vector.tensor_copy(t[:], word_pool[:].indirect(offsets[:, half * H // 16 : (half + 1) * H // 16]))
-            key_words.append(t)
+            key_words = held.tile([P, HALF], U32, name="key_words%d" % half, align_bytes=MX_ALIGN)
+            listed = offsets[:, half * HALF // LIST_ROWS : (half + 1) * HALF // LIST_ROWS]
+            nc.vector.tensor_copy(key_words[:], word_pool[:].indirect(listed))
+            keys.append((key_words[:], key_scales[:, half * HALF : (half + 1) * HALF]))
 
-        scores = []
-        for name, t in zip(("q", "dq"), raw):
-            grouped = held.tile([P, Q, PACK], BF16, name=name + "_grouped", align_bytes=64)
+        def score(raw, name, halves):
+            grouped = held.tile([P, Q, PACK], BF16, name=name + "_grouped", align_bytes=MX_ALIGN)
             nc.scalar.copy(
-                grouped[:].rearrange("p (c i) t -> p c t i", i=4),
-                t[:].rearrange("p t (c i) -> p c t i", i=4),
+                grouped[:].rearrange("p (c n) r -> p c r n", n=4),
+                raw[:].rearrange("p r (c n) -> p c r n", n=4),
             )
-            codes = held.tile([P, Q], U32, name=name + "_codes", align_bytes=64)
-            scales = held.tile([P, Q], U8, name=name + "_scales", align_bytes=64)
-            nc.vector.quantize_mx(codes[:].bitcast(FP8X4), scales[:], grouped[:].rearrange("p w j -> p (w j)"))
-            if name == "q":
-                halves = [psum.tile([P, H], F32, name="a%d" % n, tag="bank%d" % n)[:] for n in range(2)]
-                scores.extend(b.rearrange("p (s r) -> p r s", r=PACK) for b in halves)
-            else:
-                bank = psum.tile([P, I], F32, name="ta", tag="bank2")
-                halves = [bank[:, n * H : (n + 1) * H] for n in range(2)]
-                scores.append(bank[:].rearrange("p (s r) -> p r s", r=PACK))
-            for n in range(2):
-                nc.tensor.matmul_mx(
-                    out=halves[n], lhsT=codes[:].bitcast(FP8X4), lhsT_scale=scales[:],
-                    rhs=key_words[n][:].bitcast(FP8X4), rhs_scale=key_scales[:, n * H : (n + 1) * H],
-                    start=True, stop=True,
-                )
-        a0, a1, ta = scores
+            codes = held.tile([P, Q], U32, name=name + "_codes", align_bytes=MX_ALIGN)
+            rows = quantise(codes[:], grouped[:], name)
+            for half in range(2):
+                product(halves[half], rows, keys[half])
 
-        val_pools = []
-        for j in range(E // P):
-            t = held.tile([P, T], F32, name="val_pool%d" % j, tag="slot%d" % j, align_bytes=64)
-            nc.sync.dma_start(t[:], vals[j * P : (j + 1) * P, :])
-            val_pools.append(t)
+        a_banks = [psum.tile([P, HALF], F32, name="a%d" % half, tag="bank%d" % half) for half in range(2)]
+        score(query_raw, "query", [bank[:] for bank in a_banks])
+        ta_bank = psum.tile([P, I], F32, name="ta", tag="bank2")
+        score(dquery_raw, "dquery", [ta_bank[:, 0:HALF], ta_bank[:, HALF:I]])
+        ta = ta_bank[:].rearrange("q (s r) -> q r s", r=PACK)
+
+        factor = column("factor", PACK)
+        value_pools = []
+        for j in range(VALUE_TILES):
+            pool = held.tile([P, T], F32, name="value_pool%d" % j, tag="value_pool%d" % j, align_bytes=MX_ALIGN)
+            nc.sync.dma_start(pool[:], vals[j * P : (j + 1) * P, :])
+            value_pools.append(pool)
             if j == 0:
-                nc.sync.dma_start(factor[:], slot_factor.rearrange("o (p t) -> (o p) t", t=PACK))
-
-        def wide(name):
-            return held.tile([P, PACK, P], F32, name=name)
-
-        def col(name, n=1):
-            return held.tile([P, n], F32, name=name)
+                nc.sync.dma_start(factor[:], slot_factor.rearrange("o (s r) -> (o s) r", r=PACK))
 
         def turn_values(j, grouped, tag):
-            picked = held.tile([P, I], BF16, name="picked%d" % j, tag=tag, align_bytes=64)
-            nc.vector.tensor_copy(picked[:], val_pools[j][:].indirect(offsets[:]))
-            words = picked[:].bitcast(F32)
+            picked = held.tile([P, I], BF16, name="picked%d" % j, tag=tag, align_bytes=MX_ALIGN)
+            nc.vector.tensor_copy(picked[:], value_pools[j][:].indirect(offsets[:]))
+            pairs = picked[:].bitcast(F32)
             turned = psum.tile([P, 2, P], F32, name="turned", tag="turned", bufs=2)
             for u in range(2):
-                nc.tensor.transpose(turned[:, u, :], words[:, u : I // 2 : 2], ident[:])
-            nc.scalar.copy(grouped.bitcast(F32), turned[:].rearrange("p u e -> p e u"))
+                nc.tensor.transpose(turned[:, u, :], pairs[:, u : I // 2 : 2], ident[:])
+            nc.scalar.copy(grouped.bitcast(F32), turned[:].rearrange("s u e -> s e u"))
 
-        def quantise(codes, grouped, name):
-            scales = held.tile([P, codes.shape[1]], U8, name=name + "_scales", align_bytes=64)
-            nc.vector.quantize_mx(codes.bitcast(FP8X4), scales[:], grouped.rearrange("p w j -> p (w j)"))
-            return codes, scales
+        gain_terms, neg_gain = column("gain_terms", 2), column("neg_gain")
+        nc.vector.tensor_scalar(gain_terms[:, 1:2], gain_col[:], float(I), None, ALU.mult)
+        nc.vector.tensor_scalar(neg_gain[:], gain_col[:], -float(I), None, ALU.mult)
 
-        c, neg_c = col("c", 2), col("neg_c")
-        nc.vector.tensor_scalar(c[:, 1:2], gain_col[:], float(I), None, ALU.mult)
-        nc.vector.tensor_scalar(neg_c[:], gain_col[:], -float(I), None, ALU.mult)
+        neg_a = dealt("neg_a")
+        neg_max = None
+        for half in range(2):
+            least = column("neg_max%d" % half)
+            nc.vector.tensor_scalar(
+                neg_a[:, :, half * P // 2 : (half + 1) * P // 2],
+                a_banks[half][:].rearrange("q (s r) -> q r s", r=PACK),
+                -1.0, neg_max, ALU.mult, ALU.min, accum_out=least[:],
+            )
+            neg_max = least[:]
+        p, z = dealt("p"), column("z")
+        nc.scalar.activation(p[:], neg_a[:], ACT.Exp, bias=neg_max, scale=-1.0, accum_out=z[:])
 
-        neg_a, neg_max0, neg_max = wide("neg_a"), col("neg_max0"), col("neg_max")
-        nc.vector.tensor_scalar(neg_a[:, :, 0 : P // 2], a0, -1.0, None, ALU.mult, ALU.min, accum_out=neg_max0[:])
-        nc.vector.tensor_scalar(neg_a[:, :, P // 2 : P], a1, -1.0, neg_max0[:], ALU.mult, ALU.min, accum_out=neg_max[:])
-        p, z = wide("p"), col("z")
-        nc.scalar.activation(p[:], neg_a[:], ACT.Exp, bias=neg_max[:], scale=-1.0, accum_out=z[:])
+        values01 = held.tile([P, 2 * P, PACK], BF16, name="values01", align_bytes=MX_ALIGN)
+        values2 = held.tile([P, P, PACK], BF16, name="values2", align_bytes=MX_ALIGN)
+        values3 = held.tile([P, P, PACK], BF16, name="values3", align_bytes=MX_ALIGN)
+        turn_values(0, values01[:, 0:P, :], "picked0")
 
-        v01 = held.tile([P, 2 * P, PACK], BF16, name="v01", align_bytes=64)
-        v2 = held.tile([P, P, PACK], BF16, name="v2", align_bytes=64)
-        v3 = held.tile([P, P, PACK], BF16, name="v3", align_bytes=64)
-        turn_values(0, v01[:, 0:P, :], "picked0")
-
-        scratch = held.tile([P, I + 8], F32, name="scratch", tag="slot0", align_bytes=64)
-        junk = scratch[:, 0:I].rearrange("p (r s) -> p r s", r=PACK)
-        rz = scratch[:, I : I + 1]
+        after_gather0 = held.tile([P, I + 8], F32, name="after_gather0", tag="value_pool0", align_bytes=MX_ALIGN)
+        neg_gain_p = after_gather0[:, 0:I].rearrange("q (r s) -> q r s", r=PACK)
+        rz = after_gather0[:, I : I + 1]
         nc.vector.reciprocal(rz, z[:])
-        nc.vector.tensor_scalar(junk, p[:], neg_c[:], None, ALU.mult, ALU.min, accum_out=c[:, 0:1])
-        nc.scalar.activation(s[:, 0:2], c[:], ACT.Identity, scale=rz)
-        p2, z2 = wide("p2"), col("z2")
-        nc.scalar.activation(p2[:], p[:], ACT.Exp, bias=s[:, 0:1], scale=s[:, 1:2], accum_out=z2[:])
+        nc.vector.tensor_scalar(neg_gain_p, p[:], neg_gain[:], None, ALU.mult, ALU.min, accum_out=gain_terms[:, 0:1])
+        nc.scalar.activation(row_terms[:, 0:2], gain_terms[:], ACT.Identity, scale=rz)
+        p2, z2 = dealt("p2"), column("z2")
+        nc.scalar.activation(p2[:], p[:], ACT.Exp, bias=row_terms[:, 0:1], scale=row_terms[:, 1:2], accum_out=z2[:])
 
-        tp, mu = wide("tp"), col("mu")
-        nc.vector.scalar_tensor_tensor(tp[:], ta, rz, p[:], ALU.mult, ALU.mult, accum_out=mu[:])
-        g = held.tile([P, PACK, P], F32, name="g", tag="g", align_bytes=64)
-        nc.vector.scalar_tensor_tensor(g[:], ta, mu[:], p[:], ALU.subtract, ALU.mult)
-        rz2, k = col("rz2"), col("k", 2)
+        tp_over_z, mu = dealt("tp_over_z"), column("mu")
+        nc.vector.scalar_tensor_tensor(tp_over_z[:], ta, rz, p[:], ALU.mult, ALU.mult, accum_out=mu[:])
+        centred = held.tile([P, PACK, P], F32, name="centred", tag="centred", align_bytes=MX_ALIGN)
+        nc.vector.scalar_tensor_tensor(centred[:], ta, mu[:], p[:], ALU.subtract, ALU.mult)
+        rz2, over_z2 = column("rz2"), column("over_z2", 2)
         nc.vector.reciprocal(rz2[:], z2[:])
-        nc.vector.tensor_scalar(k[:], s[:, 1:3], rz2[:], None, ALU.mult)
-        big, h = wide("big"), col("h")
-        nc.vector.scalar_tensor_tensor(big[:], g[:], k[:, 0:1], p2[:], ALU.mult, ALU.mult, accum_out=h[:])
-        nr = col("nr")
-        nc.scalar.activation(nr[:], h[:], ACT.Identity, scale=k[:, 1:2])
-        corr = wide("corr")
+        nc.vector.tensor_scalar(over_z2[:], row_terms[:, 1:3], rz2[:], None, ALU.mult)
+        lead, lead_sum = dealt("lead"), column("lead_sum")
+        nc.vector.scalar_tensor_tensor(lead[:], centred[:], over_z2[:, 0:1], p2[:], ALU.mult, ALU.mult, accum_out=lead_sum[:])
+        shift = column("shift")
+        nc.scalar.activation(shift[:], lead_sum[:], ACT.Identity, scale=over_z2[:, 1:2])
+
+        correction = dealt("correction")
         tw_banks = [psum.tile([P, Q], F32, name="tw%d" % r, tag="bank%d" % r) for r in range(PACK)]
         for r in range(PACK):
-            nc.tensor.matmul(tw_banks[r][:], big[:, r, :], ident[:], start=True, stop=False, is_transpose=True)
+            nc.tensor.matmul(tw_banks[r][:], lead[:, r, :], ident[:], start=True, stop=False, is_transpose=True)
         for r in range(PACK):
-            nc.scalar.activation(corr[:, r, :], p2[:, r, :], ACT.Identity, scale=nr[:])
-            nc.tensor.matmul(tw_banks[r][:], corr[:, r, :], ident[:], start=False, stop=True, is_transpose=True)
-        w_grouped = held.tile([P, Q, PACK], BF16, name="w_grouped", align_bytes=64)
+            nc.scalar.activation(correction[:, r, :], p2[:, r, :], ACT.Identity, scale=shift[:])
+            nc.tensor.matmul(tw_banks[r][:], correction[:, r, :], ident[:], start=False, stop=True, is_transpose=True)
+        weights = held.tile([P, Q, PACK], BF16, name="weights", align_bytes=MX_ALIGN)
         for r in range(PACK):
-            nc.scalar.activation(w_grouped[:, :, r], tw_banks[r][:], ACT.Identity, scale=factor[:, r : r + 1])
+            nc.scalar.activation(weights[:, :, r], tw_banks[r][:], ACT.Identity, scale=factor[:, r : r + 1])
 
-        turn_values(1, v01[:, P : 2 * P, :], "g")
-        turn_values(2, v2[:], "picked2")
-        turn_values(3, v3[:], "picked3")
-        codes = held.tile([P, 5 * P], U32, name="late_codes", tag="slot3", align_bytes=64)
-        v01_ops = quantise(codes[:, 0 : 2 * P], v01[:], "v01")
-        w_codes, w_scales = quantise(codes[:, 2 * P : 3 * P], w_grouped[:], "w")
-        v2_ops = quantise(codes[:, 3 * P : 4 * P], v2[:], "v2")
-        v3_ops = quantise(codes[:, 4 * P : 5 * P], v3[:], "v3")
+        turn_values(1, values01[:, P : 2 * P, :], "centred")
+        turn_values(2, values2[:], "picked2")
+        turn_values(3, values3[:], "picked3")
 
-        e0 = 0
-        for name, parts in (("first", (v01_ops, v2_ops)), ("last", (v3_ops,))):
+        codes = held.tile([P, Q + E], U32, name="codes", tag="value_pool3", align_bytes=MX_ALIGN)
+        values01_mx = quantise(codes[:, 0 : 2 * P], values01[:], "values01")
+        weights_mx = quantise(codes[:, 2 * P : 3 * P], weights[:], "weights")
+        values2_mx = quantise(codes[:, 3 * P : 4 * P], values2[:], "values2")
+        values3_mx = quantise(codes[:, 4 * P : 5 * P], values3[:], "values3")
+
+        stored = 0
+        for name, parts in (("first", (values01_mx, values2_mx)), ("last", (values3_mx,))):
             width = sum(part[0].shape[1] for part in parts)
             acc = psum.tile([P, width], F32, name="acc_" + name)
-            n0 = 0
-            for v_codes, v_scales in parts:
-                n1 = n0 + v_codes.shape[1]
-                nc.tensor.matmul_mx(
-                    out=acc[:, n0:n1], lhsT=w_codes.bitcast(FP8X4), lhsT_scale=w_scales[:],
-                    rhs=v_codes.bitcast(FP8X4), rhs_scale=v_scales[:], start=True, stop=True,
-                )
-                n0 = n1
+            filled = 0
+            for part in parts:
+                product(acc[:, filled : filled + part[0].shape[1]], weights_mx, part)
+                filled = filled + part[0].shape[1]
             result = held.tile([P, width], F32, name="result_" + name)
             nc.scalar.copy(result[:], acc[:])
-            nc.sync.dma_start(out[:, e0 : e0 + width], result[:])
-            e0 = e0 + width
+            nc.sync.dma_start(out[:, stored : stored + width], result[:])
+            stored = stored + width

from contextlib import ExitStack

import concourse.mybir as mybir
from concourse.masks import make_identity

D, E, T, I, Q = 512, 512, 2048, 512, 128
FLOPS = 2 * (2 * D * Q * I + I * Q * E)

F32 = mybir.dt.float32
BF16 = mybir.dt.bfloat16
I32 = mybir.dt.int32
U32 = mybir.dt.uint32
U16 = mybir.dt.uint16
U8 = mybir.dt.uint8
FP8X4 = mybir.dt.float8_e4m3fn_x4
ALU = mybir.AluOpType
ACT = mybir.ActivationFunctionType

P = 128
PACK = 4
QUADRANT = 32
LIST_ROWS = 16
HALF = I // 2
VALUE_TILES = E // P
MX_ALIGN = 64


def tile_attend_ttdoubled_kernel(tc, query, keys_words, keys_scales, gain, dquery, slot_factor, vals, offs, out):
    nc = tc.nc
    with ExitStack() as ctx:
        held = ctx.enter_context(tc.tile_pool(name="held", bufs=1))
        psum = ctx.enter_context(tc.psum_pool(name="psum", bufs=1))

        def dealt(name):
            return held.tile([P, PACK, P], F32, name=name)

        def column(name, n=1):
            return held.tile([P, n], F32, name=name)

        def quantise(codes, grouped, name):
            scales = held.tile([P, codes.shape[1]], U8, name=name + "_scales", align_bytes=MX_ALIGN)
            nc.vector.quantize_mx(codes.bitcast(FP8X4), scales[:], grouped.rearrange("p c r -> p (c r)"))
            return codes, scales[:]

        def product(acc, stationary, moving):
            nc.tensor.matmul_mx(
                out=acc, lhsT=stationary[0].bitcast(FP8X4), lhsT_scale=stationary[1],
                rhs=moving[0].bitcast(FP8X4), rhs_scale=moving[1], start=True, stop=True,
            )

        scale_rows = held.tile([P, T // 4], I32, name="scale_rows")
        for quad in range(P // QUADRANT):
            (nc.sync, nc.scalar)[quad % 2].dma_start(
                scale_rows[QUADRANT * quad : QUADRANT * quad + 4, :],
                keys_scales[0, 4 * quad : 4 * quad + 4, :].bitcast(I32),
            )
        offsets = held.tile([P, I // LIST_ROWS], U16, name="offsets")
        nc.sync.dma_start(offsets[:], offs)

        scale_pool = held.tile([P, T], U8, name="scale_pool")
        nc.vector.memset(scale_pool[:].bitcast(I32), 0)
        for quad in range(P // QUADRANT):
            rows = slice(QUADRANT * quad, QUADRANT * quad + 4)
            nc.vector.tensor_copy(scale_pool[rows, :].bitcast(I32), scale_rows[rows, :])

        query_raw = held.tile([P, PACK, Q], F32, name="query_raw")
        nc.sync.dma_start(query_raw[:], query.rearrange("(p r) c -> p r c", r=PACK))
        word_pool = held.tile([P, T], U32, name="word_pool")
        nc.sync.dma_start(word_pool[:].bitcast(I32), keys_words[0].rearrange("p n r -> p (n r)").bitcast(I32))
        dquery_raw = held.tile([P, PACK, Q], F32, name="dquery_raw")
        nc.sync.dma_start(dquery_raw[:], dquery.rearrange("(p r) c -> p r c", r=PACK))
        gain_col = column("gain_col")
        nc.sync.dma_start(gain_col[:], gain)

        ident = held.tile([P, P], F32, name="ident")
        make_identity(nc, ident[:])

        row_terms = column("row_terms", 3)
        nc.vector.memset(row_terms[:, 2:3], -1.0)

        key_scales = held.tile([P, I], U8, name="key_scales", align_bytes=MX_ALIGN)
        nc.vector.tensor_copy(key_scales[:], scale_pool[:].indirect(offsets[:]))
        keys = []
        for half in range(2):
            key_words = held.tile([P, HALF], U32, name="key_words%d" % half, align_bytes=MX_ALIGN)
            listed = offsets[:, half * HALF // LIST_ROWS : (half + 1) * HALF // LIST_ROWS]
            nc.vector.tensor_copy(key_words[:], word_pool[:].indirect(listed))
            keys.append((key_words[:], key_scales[:, half * HALF : (half + 1) * HALF]))

        def score(raw, name, halves):
            grouped = held.tile([P, Q, PACK], BF16, name=name + "_grouped", align_bytes=MX_ALIGN)
            nc.scalar.copy(
                grouped[:].rearrange("p (c n) r -> p c r n", n=4),
                raw[:].rearrange("p r (c n) -> p c r n", n=4),
            )
            codes = held.tile([P, Q], U32, name=name + "_codes", align_bytes=MX_ALIGN)
            rows = quantise(codes[:], grouped[:], name)
            for half in range(2):
                product(halves[half], rows, keys[half])

        a_banks = [psum.tile([P, HALF], F32, name="a%d" % half, tag="bank%d" % half) for half in range(2)]
        score(query_raw, "query", [bank[:] for bank in a_banks])
        ta_bank = psum.tile([P, I], F32, name="ta", tag="bank2")
        score(dquery_raw, "dquery", [ta_bank[:, 0:HALF], ta_bank[:, HALF:I]])
        ta = ta_bank[:].rearrange("q (s r) -> q r s", r=PACK)

        factor = column("factor", PACK)
        value_pools = []
        for j in range(VALUE_TILES):
            pool = held.tile([P, T], F32, name="value_pool%d" % j, tag="value_pool%d" % j, align_bytes=MX_ALIGN)
            nc.sync.dma_start(pool[:], vals[j * P : (j + 1) * P, :])
            value_pools.append(pool)
            if j == 0:
                nc.sync.dma_start(factor[:], slot_factor.rearrange("o (s r) -> (o s) r", r=PACK))

        def turn_values(j, grouped, tag):
            picked = held.tile([P, I], BF16, name="picked%d" % j, tag=tag, align_bytes=MX_ALIGN)
            nc.vector.tensor_copy(picked[:], value_pools[j][:].indirect(offsets[:]))
            pairs = picked[:].bitcast(F32)
            turned = psum.tile([P, 2, P], F32, name="turned", tag="turned", bufs=2)
            for u in range(2):
                nc.tensor.transpose(turned[:, u, :], pairs[:, u : I // 2 : 2], ident[:])
            nc.scalar.copy(grouped.bitcast(F32), turned[:].rearrange("s u e -> s e u"))

        gain_terms, neg_gain = column("gain_terms", 2), column("neg_gain")
        nc.vector.tensor_scalar(gain_terms[:, 1:2], gain_col[:], float(I), None, ALU.mult)
        nc.vector.tensor_scalar(neg_gain[:], gain_col[:], -float(I), None, ALU.mult)

        neg_a = dealt("neg_a")
        neg_max = None
        for half in range(2):
            least = column("neg_max%d" % half)
            nc.vector.tensor_scalar(
                neg_a[:, :, half * P // 2 : (half + 1) * P // 2],
                a_banks[half][:].rearrange("q (s r) -> q r s", r=PACK),
                -1.0, neg_max, ALU.mult, ALU.min, accum_out=least[:],
            )
            neg_max = least[:]
        p, z = dealt("p"), column("z")
        nc.scalar.activation(p[:], neg_a[:], ACT.Exp, bias=neg_max, scale=-1.0, accum_out=z[:])

        values01 = held.tile([P, 2 * P, PACK], BF16, name="values01", align_bytes=MX_ALIGN)
        values2 = held.tile([P, P, PACK], BF16, name="values2", align_bytes=MX_ALIGN)
        values3 = held.tile([P, P, PACK], BF16, name="values3", align_bytes=MX_ALIGN)
        turn_values(0, values01[:, 0:P, :], "picked0")

        after_gather0 = held.tile([P, I + 8], F32, name="after_gather0", tag="value_pool0", align_bytes=MX_ALIGN)
        neg_gain_p = after_gather0[:, 0:I].rearrange("q (r s) -> q r s", r=PACK)
        rz = after_gather0[:, I : I + 1]
        nc.vector.reciprocal(rz, z[:])
        nc.vector.tensor_scalar(neg_gain_p, p[:], neg_gain[:], None, ALU.mult, ALU.min, accum_out=gain_terms[:, 0:1])
        nc.scalar.activation(row_terms[:, 0:2], gain_terms[:], ACT.Identity, scale=rz)
        p2, z2 = dealt("p2"), column("z2")
        nc.scalar.activation(p2[:], p[:], ACT.Exp, bias=row_terms[:, 0:1], scale=row_terms[:, 1:2], accum_out=z2[:])

        tp_over_z, mu = dealt("tp_over_z"), column("mu")
        nc.vector.scalar_tensor_tensor(tp_over_z[:], ta, rz, p[:], ALU.mult, ALU.mult, accum_out=mu[:])
        centred = held.tile([P, PACK, P], F32, name="centred", tag="centred", align_bytes=MX_ALIGN)
        nc.vector.scalar_tensor_tensor(centred[:], ta, mu[:], p[:], ALU.subtract, ALU.mult)
        rz2, over_z2 = column("rz2"), column("over_z2", 2)
        nc.vector.reciprocal(rz2[:], z2[:])
        nc.vector.tensor_scalar(over_z2[:], row_terms[:, 1:3], rz2[:], None, ALU.mult)
        lead, lead_sum = dealt("lead"), column("lead_sum")
        nc.vector.scalar_tensor_tensor(lead[:], centred[:], over_z2[:, 0:1], p2[:], ALU.mult, ALU.mult, accum_out=lead_sum[:])
        shift = column("shift")
        nc.scalar.activation(shift[:], lead_sum[:], ACT.Identity, scale=over_z2[:, 1:2])

        correction = dealt("correction")
        tw_banks = [psum.tile([P, Q], F32, name="tw%d" % r, tag="bank%d" % r) for r in range(PACK)]
        for r in range(PACK):
            nc.tensor.matmul(tw_banks[r][:], lead[:, r, :], ident[:], start=True, stop=False, is_transpose=True)
        for r in range(PACK):
            nc.scalar.activation(correction[:, r, :], p2[:, r, :], ACT.Identity, scale=shift[:])
            nc.tensor.matmul(tw_banks[r][:], correction[:, r, :], ident[:], start=False, stop=True, is_transpose=True)
        weights = held.tile([P, Q, PACK], BF16, name="weights", align_bytes=MX_ALIGN)
        for r in range(PACK):
            nc.scalar.activation(weights[:, :, r], tw_banks[r][:], ACT.Identity, scale=factor[:, r : r + 1])

        turn_values(1, values01[:, P : 2 * P, :], "centred")
        turn_values(2, values2[:], "picked2")
        turn_values(3, values3[:], "picked3")

        codes = held.tile([P, Q + E], U32, name="codes", tag="value_pool3", align_bytes=MX_ALIGN)
        values01_mx = quantise(codes[:, 0 : 2 * P], values01[:], "values01")
        weights_mx = quantise(codes[:, 2 * P : 3 * P], weights[:], "weights")
        values2_mx = quantise(codes[:, 3 * P : 4 * P], values2[:], "values2")
        values3_mx = quantise(codes[:, 4 * P : 5 * P], values3[:], "values3")

        stored = 0
        for name, parts in (("first", (values01_mx, values2_mx)), ("last", (values3_mx,))):
            width = sum(part[0].shape[1] for part in parts)
            acc = psum.tile([P, width], F32, name="acc_" + name)
            filled = 0
            for part in parts:
                product(acc[:, filled : filled + part[0].shape[1]], weights_mx, part)
                filled = filled + part[0].shape[1]
            result = held.tile([P, width], F32, name="result_" + name)
            nc.scalar.copy(result[:], acc[:])
            nc.sync.dma_start(out[:, stored : stored + width], result[:])
            stored = stored + width
